import numpy as np, ml_dtypes
CORES = [21,109,149,237,277,365,405,493,150,406]
N = 10
import mx_ref
NC, WT = 128, 1
LR = np.float32(2.0 ** -3)
BF = ml_dtypes.bfloat16
def cut(t, i, w=512):
    return t[:, w * i:w * i + w]
def setup_inputs(rng):
    def f(*shape):
        return mx_ref.flush((rng.standard_normal(shape, dtype=np.float32) * np.exp2(rng.integers(-2, 3, shape[:-1] + (1,)))).astype(BF))
    return {"w": f(N, 128, WT * 512), "gr": f(N, 128, WT * 512), "x": f(N, 128, 4 * NC)}
def setup_inputs_blocks(rng):
    d = setup_inputs(rng)
    for k in ("x",): d[k] = mx_ref.spread(d[k], rng, 4)
    for k in ("w", "gr"): d[k] = mx_ref.spread(d[k], rng, 2)
    return d
def setup_inputs_wide(rng):
    d = setup_inputs(rng)
    for k in ("w", "gr", "x"): d[k] = mx_ref.flush((d[k].astype(np.float32) * np.exp2(rng.integers(-4, 5, (N, 1, 1))).astype(np.float32)).astype(BF))
    return d
def setup_inputs_faint(rng):
    d = setup_inputs(rng); d["gr"] = mx_ref.flush((d["gr"].astype(np.float32) * np.float32(2.0 ** -12)).astype(BF))
    return d
def reference(w, gr, x):
    H = [mx_ref.quantize((cut(w[j], i).astype(np.float32) - cut(gr[j], i).astype(np.float32) * LR).astype(BF)) for j in range(N) for i in range(WT)]
    y = np.zeros((N, 128, N * WT * NC), np.float32)
    for r in range(N):
        X = mx_ref.quantize(x[r])
        for b in range(N * WT):
            y[r][:, NC * b:NC * b + NC] = mx_ref.matmul(H[b], X)
    return {"y": y}

@@ -1,0 +1,208 @@
+from concourse.bass import DstId, RemoteDMATransfer
+from concourse.mybir import dt, AluOpType
+
+N = 10
+NC = 128
+ALL_CORES = 512
+BANK = 512
+BANKS = 8
+HUB_FAN = 3
+
+SCRATCH = {
+    "wt": ("sbuf", [128, 4 * NC], "bfloat16"),
+    "gt": ("sbuf", [128, 4 * NC], "bfloat16"),
+    "gs": ("sbuf", [128, 4 * NC], "bfloat16"),
+    "vt": ("sbuf", [128, 4 * NC], "bfloat16"),
+    "xt": ("sbuf", [128, 4 * NC], "bfloat16"),
+    "xq": ("sbuf", [128, NC], "float8_e4m3fn_x4"),
+    "xs": ("sbuf", [128, NC], "uint8"),
+    "cq": ("sbuf", [128, N * NC], "float8_e4m3fn_x4"),
+    "cs": ("sbuf", [128, N * NC], "uint8"),
+    "yt": ("sbuf", [128, N * NC], "float32"),
+    "ps": ("psum", [128, BANKS * BANK], "float32"),
+}
+SEMAPHORES = (["ldw", "ldg", "ldx", "scaled", "made", "packed", "xpacked", "sent", "st0", "st1"]
+              + ["c%d" % j for j in range(N)] + ["s%d" % j for j in range(N)]
+              + ["mm%d" % j for j in range(N)] + ["cp%d" % j for j in range(N)])
+
+
+def build_plan(T, topo):
+    C = list(T.cores)
+
+    def same_chip(a, b):
+        return topo.host(a) == topo.host(b) and topo.chip(a) == topo.chip(b)
+
+    def same_rack(a, b):
+        return topo.rack(topo.host(a)) == topo.rack(topo.host(b))
+
+    chip_cores = {c: [d for d in range(ALL_CORES) if same_chip(c, d)] for c in C}
+    sib = [[d for d in C if d != c and same_chip(c, d)] for c in C]
+    plane = [[d for d in C if topo.same_plane(c, d)] for c in C]
+    cross = [[d for d in C if same_rack(c, d) and not same_chip(c, d) and not topo.same_plane(c, d)] for c in C]
+    land = [min(q for q in range(N) if not same_rack(c, C[q]) and topo.chip(c) == topo.chip(C[q])
+                and topo.may_write(c, C[q])) for c in C]
+    used = set(C)
+
+    def hub(r, same_die):
+        for d in chip_cores[C[r]]:
+            if d not in used and (topo.die(d) == topo.die(C[r])) == same_die and \
+                    all(topo.may_write(d, e) for e in cross[r]):
+                used.add(d)
+                return d
+
+    near = [None if all(topo.may_write(C[t], e) for e in cross[t]) else hub(t, True) for t in range(N)]
+    far = [hub(land[t], False) for t in range(N)]
+    far_dst, land_dst = [], []
+    for t in range(N):
+        q = land[t]
+        room = max(0, HUB_FAN - len(cross[q]))
+        k = max(0, len(plane[q]) - room)
+        far_dst.append(cross[q] + plane[q][k:])
+        land_dst.append(plane[q][:k])
+    slots = sorted(range(N), key=lambda t: (land[t], t))
+    slot = [slots.index(t) for t in range(N)]
+    return dict(C=C, sib=sib, plane=plane, cross=cross, land=land, near=near, far=far, far_dst=far_dst,
+                land_dst=land_dst, slot=slot)
+
+
+def rank_program(g, core, T, topo):
+    P = build_plan(T, topo)
+    C, slot = P["C"], P["slot"]
+    rank = T.rank_of(core)
+    sent = [0]
+
+    def span(tiles):
+        a = min(slot[t] for t in tiles)
+        return a * NC, (a + len(tiles)) * NC
+
+    def mask_of(dsts):
+        m = topo.mask(core, dsts[0])
+        for d in dsts:
+            m &= topo.mask(core, d)
+        return m
+
+    def transfer(kind, tiles, dsts, mask):
+        a, b = span(tiles)
+        if kind == "c":
+            ap = T.cq[:, a:b].bitcast(dt.uint8)
+        else:
+            ap = T.cs[:, a:b]
+        ids = []
+        for d in dsts:
+            rid, pid = topo.addr(d, core)
+            ids.append(DstId(rid=rid, pnc=pid))
+        sent[0] += bin(mask).count("1")
+        return RemoteDMATransfer(dst_ids=ids, dma_engine_mask=mask, remote_sem=T.sem["%s%d" % (kind, tiles[0])],
+                                 srcs=[ap], dsts=[ap for _ in dsts])
+
+    def send(kind, tiles, groups):
+        g.remote_dma_fused([transfer(kind, tiles, d, m) for d, m in groups], local_sem=T.sem.sent)
+
+    def arrivals(t, dst):
+        q = P["land"][t]
+        if dst in P["land_dst"][t]:
+            first = min(u for u in range(N) if P["land"][u] == q)
+            return first, bin(topo.mask(C[q], dst)).count("1")
+        if dst in P["sib"][q]:
+            return t, bin(topo.mask(C[q], dst)).count("1")
+        if dst in P["far_dst"][t]:
+            return t, bin(topo.mask(P["far"][t], dst)).count("1")
+        if dst == P["near"][t] or dst in P["sib"][t]:
+            return t, bin(topo.mask(C[t], dst) & ~topo.mask(C[t], P["far"][t])).count("1")
+        if P["near"][t] is not None and dst in P["cross"][t]:
+            return t, bin(topo.mask(P["near"][t], dst)).count("1")
+        return t, bin(topo.mask(C[t], dst)).count("1")
+
+    def wait(queue, kind, t):
+        first, n = arrivals(t, core)
+        queue.wait_ge(T.sem["%s%d" % (kind, first)], n)
+
+    for t in range(N):
+        if core in (P["near"][t], P["far"][t]):
+            dsts = P["cross"][t] if core == P["near"][t] else P["far_dst"][t]
+            m = mask_of(dsts)
+            for kind in ("c", "s"):
+                wait(g, kind, t)
+                send(kind, [t], [(dsts, m)])
+    if rank is None:
+        if sent[0]:
+            g.wait_ge(T.sem.sent, sent[0])
+        return
+
+    g.sync.dma_start(T.gt[:], T.gr[:]).then_inc(T.sem.ldg, 16)
+    g.scalar.dma_start(T.wt[:], T.w[:]).then_inc(T.sem.ldw, 16)
+    g.sync.wait_ge(T.sem.ldg, 16)
+    g.sync.dma_start(T.xt[:], T.x[:]).then_inc(T.sem.ldx, 16)
+
+    a, b = span([rank])
+    g.vector.wait_ge(T.sem.ldg, 16)
+    g.vector.tensor_scalar(T.gs[:], T.gt[:], 0.125, None, AluOpType.mult).then_inc(T.sem.scaled, 1)
+    g.vector.wait_ge(T.sem.ldw, 16)
+    g.vector.wait_ge(T.sem.scaled, 1)
+    g.vector.tensor_tensor(T.vt[:], T.wt[:], T.gs[:], AluOpType.subtract).then_inc(T.sem.made, 1)
+    g.vector.wait_ge(T.sem.made, 1)
+    g.vector.quantize_mx(T.cq[:, a:b], T.cs[:, a:b], T.vt[:]).then_inc(T.sem.packed, 1)
+    g.vector.wait_ge(T.sem.ldx, 16)
+    g.vector.quantize_mx(T.xq[:], T.xs[:], T.xt[:]).then_inc(T.sem.xpacked, 1)
+
+    far = P["far"][rank]
+    off = topo.mask(core, far)
+    onchip = ([P["near"][rank]] if P["near"][rank] is not None else []) + P["sib"][rank]
+    first = [([far], off)]
+    if onchip:
+        first.append((onchip, mask_of(onchip) & ~off))
+    second = [C[P["land"][rank]]] + (P["cross"][rank] if P["near"][rank] is None else []) + P["plane"][rank]
+    g.wait_ge(T.sem.packed, 1)
+    for groups in (first, [(second, mask_of(second))]):
+        for kind in ("c", "s"):
+            send(kind, [rank], groups)
+    landed = [t for t in range(N) if P["land"][t] == rank]
+    if landed:
+        rest = P["land_dst"][landed[0]]
+        for dsts in (P["sib"][rank], rest):
+            for batch in ([[t] for t in landed] if dsts is not rest else [landed]):
+                if dsts:
+                    for kind in ("c", "s"):
+                        for t in batch:
+                            wait(g, kind, t)
+                        send(kind, batch, [(dsts, mask_of(dsts))])
+
+    def when(t):
+        if t == rank:
+            return 0
+        if C[t] in P["sib"][rank]:
+            return 1
+        if t in landed:
+            return 2
+        if C[t] in P["plane"][rank]:
+            return 3
+        if C[t] in P["cross"][rank]:
+            return 5 if P["near"][t] is not None else 4
+        return 7 if core in P["far_dst"][t] else 6
+
+    order = sorted(range(N), key=lambda t: (when(t), t))
+    g.tensor.wait_ge(T.sem.xpacked, 1)
+    for k, t in enumerate(order):
+        if t == rank:
+            g.tensor.wait_ge(T.sem.packed, 1)
+        else:
+            wait(g.tensor, "c", t)
+            wait(g.tensor, "s", t)
+        if k >= BANKS:
+            g.tensor.wait_ge(T.sem["cp%d" % (k - BANKS)], 1)
+        a, b = span([t])
+        p = BANK * (k % BANKS)
+        g.tensor.matmul_mx(T.ps[:, p:p + NC], T.cq[:, a:b], T.cs[:, a:b], T.xq[:], T.xs[:], True, True).then_inc(
+            T.sem["mm%d" % k], 1)
+    stored = [0, 0]
+    for k, t in enumerate(order):
+        p = BANK * (k % BANKS)
+        g.vector.wait_ge(T.sem["mm%d" % k], 1)
+        g.vector.tensor_copy(T.yt[:, NC * t:NC * t + NC], T.ps[:, p:p + NC]).then_inc(T.sem["cp%d" % k], 1)
+        q = (g.sync, g.scalar)[k % 2]
+        q.wait_ge(T.sem["cp%d" % k], 1)
+        q.dma_start(T.y[:, NC * t:NC * t + NC], T.yt[:, NC * t:NC * t + NC]).then_inc(T.sem["st%d" % (k % 2)], 16)
+        stored[k % 2] += 16
+    g.sync.wait_ge(T.sem.st0, stored[0])
+    g.scalar.wait_ge(T.sem.st1, stored[1])
+    g.wait_ge(T.sem.sent, sent[0])

@@ -6,7 +6,8 @@ NC = 128
 ALL_CORES = 512
 BANK = 512
 BANKS = 8
-HUB_FAN = 3
+NEAR_FAN = 2
+FAR_FAN = 3
 
 SCRATCH = {
     "wt": ("sbuf", [128, 4 * NC], "bfloat16"),
@@ -24,6 +25,8 @@ SCRATCH = {
 SEMAPHORES = (["ldw", "ldg", "ldx", "scaled", "made", "packed", "xpacked", "sent", "st0", "st1"]
               + ["c%d" % j for j in range(N)] + ["s%d" % j for j in range(N)]
               + ["mm%d" % j for j in range(N)] + ["cp%d" % j for j in range(N)])
+KINDS = ("s", "c")
+CACHE = {}
 
 
 def build_plan(T, topo):
@@ -43,142 +46,122 @@ def build_plan(T, topo):
                 and topo.may_write(c, C[q])) for c in C]
     used = set(C)
 
-    def hub(r, same_die):
-        for d in chip_cores[C[r]]:
-            if d not in used and (topo.die(d) == topo.die(C[r])) == same_die and \
-                    all(topo.may_write(d, e) for e in cross[r]):
-                used.add(d)
-                return d
+    def hub(r, same_die, dsts):
+        for want in (same_die, not same_die):
+            for d in chip_cores[C[r]]:
+                if d not in used and (topo.die(d) == topo.die(C[r])) == want and \
+                        all(topo.may_write(d, e) for e in dsts):
+                    used.add(d)
+                    return d
 
-    near = [None if all(topo.may_write(C[t], e) for e in cross[t]) else hub(t, True) for t in range(N)]
-    far = [hub(land[t], False) for t in range(N)]
-    far_dst, land_dst = [], []
+    near = [[] for _ in C]
+    for t in range(N):
+        for i in range(0, len(cross[t]), NEAR_FAN):
+            part = cross[t][i:i + NEAR_FAN]
+            near[t].append((hub(t, True, part), part))
+    far = [hub(land[t], False, cross[land[t]]) for t in range(N)]
+    far_dst, rest = [], []
     for t in range(N):
         q = land[t]
-        room = max(0, HUB_FAN - len(cross[q]))
-        k = max(0, len(plane[q]) - room)
-        far_dst.append(cross[q] + plane[q][k:])
-        land_dst.append(plane[q][:k])
-    slots = sorted(range(N), key=lambda t: (land[t], t))
-    slot = [slots.index(t) for t in range(N)]
-    return dict(C=C, sib=sib, plane=plane, cross=cross, land=land, near=near, far=far, far_dst=far_dst,
-                land_dst=land_dst, slot=slot)
+        every = cross[q][::-1] + plane[q]
+        far_dst.append(every[:FAR_FAN])
+        rest.append(every[FAR_FAN:])
+    helper = [[hub(land[t], True, rest[t])] if rest[t] else [] for t in range(N)]
+
+    sends, arr = {}, {}
+
+    def mask_of(src, dsts):
+        m = topo.mask(src, dsts[0])
+        for d in dsts:
+            m &= topo.mask(src, d)
+        return m
+
+    def send(src, tile, dsts):
+        off = [d for d in dsts if not same_chip(src, d)]
+        on = [d for d in dsts if same_chip(src, d)]
+        groups = []
+        if off:
+            groups.append((off, mask_of(src, off)))
+        if on:
+            groups.append((on, mask_of(src, on) & ~(groups[0][1] if off else 0)))
+        for kind in KINDS:
+            sends.setdefault(src, []).append((kind, tile, groups))
+            for ds, m in groups:
+                for d in ds:
+                    arr[(d, kind, tile)] = bin(m).count("1")
+
+    for t in range(N):
+        q = land[t]
+        send(C[t], t, [far[t]] + [h for h, _ in near[t]] + sib[t])
+        send(C[t], t, plane[t])
+        for h, dsts in near[t]:
+            send(h, t, dsts[::-1])
+        send(far[t], t, far_dst[t] + helper[t] + [C[q]] + sib[q])
+        for h in helper[t]:
+            send(h, t, rest[t])
+    return dict(C=C, sib=sib, plane=plane, cross=cross, land=land, rest=rest, sends=sends, arr=arr)
 
 
 def rank_program(g, core, T, topo):
-    P = build_plan(T, topo)
-    C, slot = P["C"], P["slot"]
+    if "plan" not in CACHE:
+        CACHE["plan"] = build_plan(T, topo)
+    P = CACHE["plan"]
+    C = P["C"]
     rank = T.rank_of(core)
-    sent = [0]
-
-    def span(tiles):
-        a = min(slot[t] for t in tiles)
-        return a * NC, (a + len(tiles)) * NC
-
-    def mask_of(dsts):
-        m = topo.mask(core, dsts[0])
-        for d in dsts:
-            m &= topo.mask(core, d)
-        return m
-
-    def transfer(kind, tiles, dsts, mask):
-        a, b = span(tiles)
-        if kind == "c":
-            ap = T.cq[:, a:b].bitcast(dt.uint8)
-        else:
-            ap = T.cs[:, a:b]
-        ids = []
-        for d in dsts:
-            rid, pid = topo.addr(d, core)
-            ids.append(DstId(rid=rid, pnc=pid))
-        sent[0] += bin(mask).count("1")
-        return RemoteDMATransfer(dst_ids=ids, dma_engine_mask=mask, remote_sem=T.sem["%s%d" % (kind, tiles[0])],
-                                 srcs=[ap], dsts=[ap for _ in dsts])
-
-    def send(kind, tiles, groups):
-        g.remote_dma_fused([transfer(kind, tiles, d, m) for d, m in groups], local_sem=T.sem.sent)
-
-    def arrivals(t, dst):
-        q = P["land"][t]
-        if dst in P["land_dst"][t]:
-            first = min(u for u in range(N) if P["land"][u] == q)
-            return first, bin(topo.mask(C[q], dst)).count("1")
-        if dst in P["sib"][q]:
-            return t, bin(topo.mask(C[q], dst)).count("1")
-        if dst in P["far_dst"][t]:
-            return t, bin(topo.mask(P["far"][t], dst)).count("1")
-        if dst == P["near"][t] or dst in P["sib"][t]:
-            return t, bin(topo.mask(C[t], dst) & ~topo.mask(C[t], P["far"][t])).count("1")
-        if P["near"][t] is not None and dst in P["cross"][t]:
-            return t, bin(topo.mask(P["near"][t], dst)).count("1")
-        return t, bin(topo.mask(C[t], dst)).count("1")
 
     def wait(queue, kind, t):
-        first, n = arrivals(t, core)
-        queue.wait_ge(T.sem["%s%d" % (kind, first)], n)
+        queue.wait_ge(T.sem["%s%d" % (kind, t)], P["arr"][(core, kind, t)])
 
-    for t in range(N):
-        if core in (P["near"][t], P["far"][t]):
-            dsts = P["cross"][t] if core == P["near"][t] else P["far_dst"][t]
-            m = mask_of(dsts)
-            for kind in ("c", "s"):
-                wait(g, kind, t)
-                send(kind, [t], [(dsts, m)])
+    if rank is not None:
+        g.sync.dma_start(T.gt[:], T.gr[:]).then_inc(T.sem.ldg, 16)
+        g.scalar.dma_start(T.wt[:], T.w[:]).then_inc(T.sem.ldw, 16)
+        g.sync.wait_ge(T.sem.ldg, 16)
+        g.sync.dma_start(T.xt[:], T.x[:]).then_inc(T.sem.ldx, 16)
+        a, b = NC * rank, NC * rank + NC
+        g.vector.wait_ge(T.sem.ldg, 16)
+        g.vector.tensor_scalar(T.gs[:], T.gt[:], 0.125, None, AluOpType.mult).then_inc(T.sem.scaled, 1)
+        g.vector.wait_ge(T.sem.ldw, 16)
+        g.vector.wait_ge(T.sem.scaled, 1)
+        g.vector.tensor_tensor(T.vt[:], T.wt[:], T.gs[:], AluOpType.subtract).then_inc(T.sem.made, 1)
+        g.vector.wait_ge(T.sem.made, 1)
+        g.vector.quantize_mx(T.cq[:, a:b], T.cs[:, a:b], T.vt[:]).then_inc(T.sem.packed, 1)
+        g.vector.wait_ge(T.sem.ldx, 16)
+        g.vector.quantize_mx(T.xq[:], T.xs[:], T.xt[:]).then_inc(T.sem.xpacked, 1)
+        g.wait_ge(T.sem.packed, 1)
+
+    sent = 0
+    for kind, t, groups in P["sends"].get(core, []):
+        if t != rank:
+            wait(g, kind, t)
+        a, b = NC * t, NC * t + NC
+        ap = T.cq[:, a:b].bitcast(dt.uint8) if kind == "c" else T.cs[:, a:b]
+        transfers = []
+        for dsts, mask in groups:
+            ids = []
+            for d in dsts:
+                rid, pid = topo.addr(d, core)
+                ids.append(DstId(rid=rid, pnc=pid))
+            transfers.append(RemoteDMATransfer(dst_ids=ids, dma_engine_mask=mask, remote_sem=T.sem["%s%d" % (kind, t)],
+                                               srcs=[ap], dsts=[ap for _ in dsts]))
+            sent += bin(mask).count("1")
+        g.remote_dma_fused(transfers, local_sem=T.sem.sent)
     if rank is None:
-        if sent[0]:
-            g.wait_ge(T.sem.sent, sent[0])
+        if sent:
+            g.wait_ge(T.sem.sent, sent)
         return
-
-    g.sync.dma_start(T.gt[:], T.gr[:]).then_inc(T.sem.ldg, 16)
-    g.scalar.dma_start(T.wt[:], T.w[:]).then_inc(T.sem.ldw, 16)
-    g.sync.wait_ge(T.sem.ldg, 16)
-    g.sync.dma_start(T.xt[:], T.x[:]).then_inc(T.sem.ldx, 16)
-
-    a, b = span([rank])
-    g.vector.wait_ge(T.sem.ldg, 16)
-    g.vector.tensor_scalar(T.gs[:], T.gt[:], 0.125, None, AluOpType.mult).then_inc(T.sem.scaled, 1)
-    g.vector.wait_ge(T.sem.ldw, 16)
-    g.vector.wait_ge(T.sem.scaled, 1)
-    g.vector.tensor_tensor(T.vt[:], T.wt[:], T.gs[:], AluOpType.subtract).then_inc(T.sem.made, 1)
-    g.vector.wait_ge(T.sem.made, 1)
-    g.vector.quantize_mx(T.cq[:, a:b], T.cs[:, a:b], T.vt[:]).then_inc(T.sem.packed, 1)
-    g.vector.wait_ge(T.sem.ldx, 16)
-    g.vector.quantize_mx(T.xq[:], T.xs[:], T.xt[:]).then_inc(T.sem.xpacked, 1)
-
-    far = P["far"][rank]
-    off = topo.mask(core, far)
-    onchip = ([P["near"][rank]] if P["near"][rank] is not None else []) + P["sib"][rank]
-    first = [([far], off)]
-    if onchip:
-        first.append((onchip, mask_of(onchip) & ~off))
-    second = [C[P["land"][rank]]] + (P["cross"][rank] if P["near"][rank] is None else []) + P["plane"][rank]
-    g.wait_ge(T.sem.packed, 1)
-    for groups in (first, [(second, mask_of(second))]):
-        for kind in ("c", "s"):
-            send(kind, [rank], groups)
-    landed = [t for t in range(N) if P["land"][t] == rank]
-    if landed:
-        rest = P["land_dst"][landed[0]]
-        for dsts in (P["sib"][rank], rest):
-            for batch in ([[t] for t in landed] if dsts is not rest else [landed]):
-                if dsts:
-                    for kind in ("c", "s"):
-                        for t in batch:
-                            wait(g, kind, t)
-                        send(kind, batch, [(dsts, mask_of(dsts))])
 
     def when(t):
         if t == rank:
             return 0
         if C[t] in P["sib"][rank]:
             return 1
-        if t in landed:
-            return 2
         if C[t] in P["plane"][rank]:
-            return 3
+            return 2
         if C[t] in P["cross"][rank]:
-            return 5 if P["near"][t] is not None else 4
-        return 7 if core in P["far_dst"][t] else 6
+            return 3
+        if P["land"][t] == rank:
+            return 4
+        return 6 if core in P["rest"][t] else 5
 
     order = sorted(range(N), key=lambda t: (when(t), t))
     g.tensor.wait_ge(T.sem.xpacked, 1)
@@ -186,23 +169,22 @@ def rank_program(g, core, T, topo):
         if t == rank:
             g.tensor.wait_ge(T.sem.packed, 1)
         else:
-            wait(g.tensor, "c", t)
-            wait(g.tensor, "s", t)
+            for kind in KINDS:
+                wait(g.tensor, kind, t)
         if k >= BANKS:
             g.tensor.wait_ge(T.sem["cp%d" % (k - BANKS)], 1)
-        a, b = span([t])
-        p = BANK * (k % BANKS)
+        a, b, p = NC * t, NC * t + NC, BANK * (k % BANKS)
         g.tensor.matmul_mx(T.ps[:, p:p + NC], T.cq[:, a:b], T.cs[:, a:b], T.xq[:], T.xs[:], True, True).then_inc(
             T.sem["mm%d" % k], 1)
     stored = [0, 0]
     for k, t in enumerate(order):
-        p = BANK * (k % BANKS)
+        a, b, p = NC * t, NC * t + NC, BANK * (k % BANKS)
         g.vector.wait_ge(T.sem["mm%d" % k], 1)
-        g.vector.tensor_copy(T.yt[:, NC * t:NC * t + NC], T.ps[:, p:p + NC]).then_inc(T.sem["cp%d" % k], 1)
+        g.vector.tensor_copy(T.yt[:, a:b], T.ps[:, p:p + NC]).then_inc(T.sem["cp%d" % k], 1)
         q = (g.sync, g.scalar)[k % 2]
         q.wait_ge(T.sem["cp%d" % k], 1)
-        q.dma_start(T.y[:, NC * t:NC * t + NC], T.yt[:, NC * t:NC * t + NC]).then_inc(T.sem["st%d" % (k % 2)], 16)
+        q.dma_start(T.y[:, a:b], T.yt[:, a:b]).then_inc(T.sem["st%d" % (k % 2)], 16)
         stored[k % 2] += 16
     g.sync.wait_ge(T.sem.st0, stored[0])
     g.scalar.wait_ge(T.sem.st1, stored[1])
-    g.wait_ge(T.sem.sent, sent[0])
+    g.wait_ge(T.sem.sent, sent)

from concourse.bass import DstId, RemoteDMATransfer
from concourse.mybir import dt, AluOpType

N = 10
NC = 128
ALL_CORES = 512
BANK = 512
BANKS = 8
NEAR_FAN = 2
FAR_FAN = 3

SCRATCH = {
    "wt": ("sbuf", [128, 4 * NC], "bfloat16"),
    "gt": ("sbuf", [128, 4 * NC], "bfloat16"),
    "gs": ("sbuf", [128, 4 * NC], "bfloat16"),
    "vt": ("sbuf", [128, 4 * NC], "bfloat16"),
    "xt": ("sbuf", [128, 4 * NC], "bfloat16"),
    "xq": ("sbuf", [128, NC], "float8_e4m3fn_x4"),
    "xs": ("sbuf", [128, NC], "uint8"),
    "cq": ("sbuf", [128, N * NC], "float8_e4m3fn_x4"),
    "cs": ("sbuf", [128, N * NC], "uint8"),
    "yt": ("sbuf", [128, N * NC], "float32"),
    "ps": ("psum", [128, BANKS * BANK], "float32"),
}
SEMAPHORES = (["ldw", "ldg", "ldx", "scaled", "made", "packed", "xpacked", "sent", "st0", "st1"]
              + ["c%d" % j for j in range(N)] + ["s%d" % j for j in range(N)]
              + ["mm%d" % j for j in range(N)] + ["cp%d" % j for j in range(N)])
KINDS = ("s", "c")
CACHE = {}


def build_plan(T, topo):
    C = list(T.cores)

    def same_chip(a, b):
        return topo.host(a) == topo.host(b) and topo.chip(a) == topo.chip(b)

    def same_rack(a, b):
        return topo.rack(topo.host(a)) == topo.rack(topo.host(b))

    chip_cores = {c: [d for d in range(ALL_CORES) if same_chip(c, d)] for c in C}
    sib = [[d for d in C if d != c and same_chip(c, d)] for c in C]
    plane = [[d for d in C if topo.same_plane(c, d)] for c in C]
    cross = [[d for d in C if same_rack(c, d) and not same_chip(c, d) and not topo.same_plane(c, d)] for c in C]
    land = [min(q for q in range(N) if not same_rack(c, C[q]) and topo.chip(c) == topo.chip(C[q])
                and topo.may_write(c, C[q])) for c in C]
    used = set(C)

    def hub(r, same_die, dsts):
        for want in (same_die, not same_die):
            for d in chip_cores[C[r]]:
                if d not in used and (topo.die(d) == topo.die(C[r])) == want and \
                        all(topo.may_write(d, e) for e in dsts):
                    used.add(d)
                    return d

    near = [[] for _ in C]
    for t in range(N):
        for i in range(0, len(cross[t]), NEAR_FAN):
            part = cross[t][i:i + NEAR_FAN]
            near[t].append((hub(t, True, part), part))
    far = [hub(land[t], False, cross[land[t]]) for t in range(N)]
    far_dst, rest = [], []
    for t in range(N):
        q = land[t]
        every = cross[q][::-1] + plane[q]
        far_dst.append(every[:FAR_FAN])
        rest.append(every[FAR_FAN:])
    helper = [[hub(land[t], True, rest[t])] if rest[t] else [] for t in range(N)]

    sends, arr = {}, {}

    def mask_of(src, dsts):
        m = topo.mask(src, dsts[0])
        for d in dsts:
            m &= topo.mask(src, d)
        return m

    def send(src, tile, dsts):
        off = [d for d in dsts if not same_chip(src, d)]
        on = [d for d in dsts if same_chip(src, d)]
        groups = []
        if off:
            groups.append((off, mask_of(src, off)))
        if on:
            groups.append((on, mask_of(src, on) & ~(groups[0][1] if off else 0)))
        for kind in KINDS:
            sends.setdefault(src, []).append((kind, tile, groups))
            for ds, m in groups:
                for d in ds:
                    arr[(d, kind, tile)] = bin(m).count("1")

    for t in range(N):
        q = land[t]
        send(C[t], t, [far[t]] + [h for h, _ in near[t]] + sib[t])
        send(C[t], t, plane[t])
        for h, dsts in near[t]:
            send(h, t, dsts[::-1])
        send(far[t], t, far_dst[t] + helper[t] + [C[q]] + sib[q])
        for h in helper[t]:
            send(h, t, rest[t])
    return dict(C=C, sib=sib, plane=plane, cross=cross, land=land, rest=rest, sends=sends, arr=arr)


def rank_program(g, core, T, topo):
    if "plan" not in CACHE:
        CACHE["plan"] = build_plan(T, topo)
    P = CACHE["plan"]
    C = P["C"]
    rank = T.rank_of(core)

    def wait(queue, kind, t):
        queue.wait_ge(T.sem["%s%d" % (kind, t)], P["arr"][(core, kind, t)])

    if rank is not None:
        g.sync.dma_start(T.gt[:], T.gr[:]).then_inc(T.sem.ldg, 16)
        g.scalar.dma_start(T.wt[:], T.w[:]).then_inc(T.sem.ldw, 16)
        g.sync.wait_ge(T.sem.ldg, 16)
        g.sync.dma_start(T.xt[:], T.x[:]).then_inc(T.sem.ldx, 16)
        a, b = NC * rank, NC * rank + NC
        g.vector.wait_ge(T.sem.ldg, 16)
        g.vector.tensor_scalar(T.gs[:], T.gt[:], 0.125, None, AluOpType.mult).then_inc(T.sem.scaled, 1)
        g.vector.wait_ge(T.sem.ldw, 16)
        g.vector.wait_ge(T.sem.scaled, 1)
        g.vector.tensor_tensor(T.vt[:], T.wt[:], T.gs[:], AluOpType.subtract).then_inc(T.sem.made, 1)
        g.vector.wait_ge(T.sem.made, 1)
        g.vector.quantize_mx(T.cq[:, a:b], T.cs[:, a:b], T.vt[:]).then_inc(T.sem.packed, 1)
        g.vector.wait_ge(T.sem.ldx, 16)
        g.vector.quantize_mx(T.xq[:], T.xs[:], T.xt[:]).then_inc(T.sem.xpacked, 1)
        g.wait_ge(T.sem.packed, 1)

    sent = 0
    for kind, t, groups in P["sends"].get(core, []):
        if t != rank:
            wait(g, kind, t)
        a, b = NC * t, NC * t + NC
        ap = T.cq[:, a:b].bitcast(dt.uint8) if kind == "c" else T.cs[:, a:b]
        transfers = []
        for dsts, mask in groups:
            ids = []
            for d in dsts:
                rid, pid = topo.addr(d, core)
                ids.append(DstId(rid=rid, pnc=pid))
            transfers.append(RemoteDMATransfer(dst_ids=ids, dma_engine_mask=mask, remote_sem=T.sem["%s%d" % (kind, t)],
                                               srcs=[ap], dsts=[ap for _ in dsts]))
            sent += bin(mask).count("1")
        g.remote_dma_fused(transfers, local_sem=T.sem.sent)
    if rank is None:
        if sent:
            g.wait_ge(T.sem.sent, sent)
        return

    def when(t):
        if t == rank:
            return 0
        if C[t] in P["sib"][rank]:
            return 1
        if C[t] in P["plane"][rank]:
            return 2
        if C[t] in P["cross"][rank]:
            return 3
        if P["land"][t] == rank:
            return 4
        return 6 if core in P["rest"][t] else 5

    order = sorted(range(N), key=lambda t: (when(t), t))
    g.tensor.wait_ge(T.sem.xpacked, 1)
    for k, t in enumerate(order):
        if t == rank:
            g.tensor.wait_ge(T.sem.packed, 1)
        else:
            for kind in KINDS:
                wait(g.tensor, kind, t)
        if k >= BANKS:
            g.tensor.wait_ge(T.sem["cp%d" % (k - BANKS)], 1)
        a, b, p = NC * t, NC * t + NC, BANK * (k % BANKS)
        g.tensor.matmul_mx(T.ps[:, p:p + NC], T.cq[:, a:b], T.cs[:, a:b], T.xq[:], T.xs[:], True, True).then_inc(
            T.sem["mm%d" % k], 1)
    stored = [0, 0]
    for k, t in enumerate(order):
        a, b, p = NC * t, NC * t + NC, BANK * (k % BANKS)
        g.vector.wait_ge(T.sem["mm%d" % k], 1)
        g.vector.tensor_copy(T.yt[:, a:b], T.ps[:, p:p + NC]).then_inc(T.sem["cp%d" % k], 1)
        q = (g.sync, g.scalar)[k % 2]
        q.wait_ge(T.sem["cp%d" % k], 1)
        q.dma_start(T.y[:, a:b], T.yt[:, a:b]).then_inc(T.sem["st%d" % (k % 2)], 16)
        stored[k % 2] += 16
    g.sync.wait_ge(T.sem.st0, stored[0])
    g.scalar.wait_ge(T.sem.st1, stored[1])
    g.wait_ge(T.sem.sent, sent)
